import numpy as np
import ml_dtypes


def mxq(x, axis, fmt="e4m3"):
    dtype, down = {"e4m3": (ml_dtypes.float8_e4m3fn, 7), "e5m2": (ml_dtypes.float8_e5m2, 14)}[fmt]
    v = np.moveaxis(np.asarray(x, np.float32).astype(ml_dtypes.bfloat16).astype(np.float64), axis, -1)
    blocks = v.reshape(v.shape[:-1] + (-1, 32))
    amax = np.abs(blocks).max(-1, keepdims=True)
    byte = np.maximum(np.where(amax > 0, np.frexp(amax)[1] - 1 + 127, 0) - down, 1)
    scale = np.exp2(byte - 127.0)
    codes = (blocks / scale).astype(np.float32).astype(dtype).astype(np.float64)
    return np.moveaxis((codes * scale).reshape(v.shape), -1, axis)


WIDE = False


def mx_kscale(k):
    if not WIDE:
        return np.ones(k)
    levels = np.array([30, -30])
    if k % 512:
        return np.exp2(np.random.permutation(np.resize(levels, k // 32))).repeat(32)
    a = np.empty((k // 512, 16))
    for p in range(k // 512):
        a[p, :8] = np.random.permutation(np.resize(levels, 8))
        for g in range(8):
            far = levels[np.abs(levels - a[p, g]) >= 10]
            a[p, g + 8] = far[np.random.randint(len(far))]
    return np.exp2(a.ravel()).repeat(32)


def f64(x):
    return np.asarray(x).astype(np.float64)


def striped(idx):
    return np.tile(np.asarray(idx).reshape(-1, 16).T, (8, 1)).astype(np.uint16)


def unstriped(offs):
    return offs[:16].T.reshape(-1).astype(np.int64)


def striped8(idx):
    return np.asarray(idx).reshape(8, -1, 16).transpose(0, 2, 1).reshape(128, -1).astype(np.uint16)


def unstriped8(offs):
    return offs.reshape(8, 16, -1).transpose(0, 2, 1).reshape(8, -1).astype(np.int64)


def pick8(x, idx, run):
    r = np.arange(len(x))
    return x[r[:, None], idx[r % (8 * run) // run]]


E2M1 = np.array([0.0, 0.5, 1.0, 1.5, 2.0, 3.0, 4.0, 6.0, -0.0, -0.5, -1.0, -1.5, -2.0, -3.0, -4.0, -6.0])


def pack_weight(w, fmt):
    k, n = w.shape
    w = f64(np.asarray(w, np.float32).astype(ml_dtypes.bfloat16)).reshape(k // 32, 32, n)
    amax = np.abs(w).max(1)
    if fmt == "e4m3":
        byte = np.frexp(amax)[1] - 1 + 127 - 7
    else:
        mant, ex = np.frexp(amax / 6.0)
        byte = np.where(mant > 0.5, ex, ex - 1) + 127
    byte = np.clip(np.where(amax > 0, byte, 1), 1, 254)
    scaled = (w * np.exp2(127.0 - byte)[:, None, :]).reshape(k, n).astype(np.float32)
    by_word = np.ascontiguousarray(scaled.reshape(k // 512, 128, 4, n).transpose(0, 1, 3, 2))
    if fmt == "e4m3":
        words = by_word.astype(ml_dtypes.float8_e4m3fn).view(np.uint8)
    else:
        c = by_word.astype(ml_dtypes.float4_e2m1fn).view(np.uint8) & 0xF
        words = (c[..., 0::2] | (c[..., 1::2] << 4)).reshape(k // 512, 128, 2 * n)
    return np.ascontiguousarray(words), np.ascontiguousarray(byte.astype(np.uint8).reshape(k // 512, 16, n))


def unpack_weight(words, scales, fmt):
    g, _, n = scales.shape
    words = np.ascontiguousarray(words).reshape(g, 128, n, -1)
    if fmt == "e4m3":
        vals = words.view(ml_dtypes.float8_e4m3fn).astype(np.float64)
    else:
        nib = np.empty((g, 128, n, 4), np.uint8)
        nib[..., 0::2] = words & 0xF
        nib[..., 1::2] = words >> 4
        vals = E2M1[nib]
    vals = vals * np.repeat(np.exp2(scales.astype(np.float64) - 127.0), 8, axis=1)[..., None]
    return vals.transpose(0, 1, 3, 2).reshape(g * 512, n)


K, T, J, R, C, S, U, E = 512, 1024, 256, 512, 512, 1024, 256, 512


def setup_inputs():
    n = np.random.standard_normal
    idx = np.random.permutation(T)[:J]
    idx2 = np.stack([np.random.permutation(C)[:J] for _ in range(8)])
    idx3 = np.random.permutation(S)[:U]
    idx4 = np.random.permutation(E)[:U]
    fk = mx_kscale(K)
    fr = mx_kscale(R)
    xtp = pack_weight(n((K, T)) / fk[:, None], "e2m1")
    wp = pack_weight(n((K, R)) * 1 / np.sqrt(K) * fk[:, None] * fr, "e4m3")
    vsp = pack_weight(n((R, S)) * 1 / np.sqrt(R) / fr[:, None], "e2m1")
    return {
        "xt_words": xtp[0],
        "xt_scales": xtp[1],
        "w_words": wp[0],
        "w_scales": wp[1],
        "vs_words": vsp[0],
        "vs_scales": vsp[1],
        "offs": striped(idx),
        "offs2": striped8(idx2),
        "offs3": striped(idx3),
        "offs4": striped(idx4),
    }


def reference(xt_words, xt_scales, w_words, w_scales, vs_words, vs_scales, offs, offs2, offs3, offs4):
    idx = unstriped(offs)
    idx2 = unstriped8(offs2)
    idx3 = unstriped(offs3)
    idx4 = unstriped(offs4)
    xtu = unpack_weight(xt_words, xt_scales, "e2m1")
    wu = unpack_weight(w_words, w_scales, "e4m3")
    vsu = unpack_weight(vs_words, vs_scales, "e2m1")
    xtidxg = xtu[:, idx]
    a = wu.T @ xtidxg
    pa = np.zeros((R, C))
    pa[np.arange(R)[:, None], idx2[np.arange(R) % 512 // 64]] = a
    paq = mxq(pa, 0, "e5m2")
    vsidx3g = vsu[:, idx3]
    p = paq.T @ vsidx3g
    y = np.zeros((C, E))
    y[:, idx4] = p
    return y

@@ -1,0 +1,186 @@
+from contextlib import ExitStack
+
+import concourse.mybir as mybir
+
+K, T, J, R, C, S, U, E = 512, 1024, 256, 512, 512, 1024, 256, 512
+FLOPS = 2 * K * R * J + 2 * R * C * U
+
+F32 = mybir.dt.float32
+BF16 = mybir.dt.bfloat16
+I32 = mybir.dt.int32
+U32 = mybir.dt.uint32
+U16 = mybir.dt.uint16
+U8 = mybir.dt.uint8
+E4M3 = mybir.dt.float8_e4m3fn_x4
+E5M2 = mybir.dt.float8_e5m2_x4
+E2M1 = mybir.dt.float4_e2m1fn_x4
+COPY = mybir.ActivationFunctionType.Copy
+
+P = 128
+PACK = 4
+QUAD = 32
+HALF = J // 2
+
+
+def tile_list_pagequeries_kernel(
+    tc, xt_words, xt_scales, w_words, w_scales, vs_words, vs_scales, offs, offs2, offs3, offs4, out
+):
+    nc = tc.nc
+    with ExitStack() as ctx:
+        lists = ctx.enter_context(tc.tile_pool(name="lists", bufs=1))
+        sb = ctx.enter_context(tc.tile_pool(name="sb", bufs=1))
+        psum = ctx.enter_context(tc.psum_pool(name="psum", bufs=1))
+
+        idx = lists.tile([P, J // 16], U16, name="idx")
+        idx2 = lists.tile([P, J // 16], U16, name="idx2")
+        idx3 = lists.tile([P, U // 16], U16, name="idx3")
+        idx4 = lists.tile([P, U // 16], U16, name="idx4")
+
+        xt_all = sb.tile([P, T], U16, name="xt_all", tag="reuse0", align_bytes=64)
+        xs_all = sb.tile([P, T], U8, name="xs_all", tag="reuse1", align_bytes=64)
+        w_raw = sb.tile([P, R], U32, name="w_raw", align_bytes=64)
+        ws_raw = sb.tile([P, 2, R], U8, name="ws_raw", align_bytes=64)
+        vs_all = sb.tile([P, S], U16, name="vs_all", align_bytes=64)
+        vsc_all = sb.tile([P, S], U8, name="vsc_all", align_bytes=64)
+        boards = [sb.tile([P, C], F32, name="board%d" % t) for t in range(PACK)]
+
+        nc.gpsimd.memset(ws_raw[:, 0, :].bitcast(I32), 0)
+        nc.vector.memset(xs_all[:].bitcast(I32), 0)
+
+        nc.sync.dma_start(idx[:], offs)
+        nc.sync.dma_start(xt_all[:].bitcast(I32), xt_words[0].bitcast(I32))
+        for h in range(2):
+            rows = w_scales[0, 8 * h : 8 * h + 8, :].rearrange("(a r) c -> r a c", a=2)
+            nc.sync.dma_start(ws_raw[64 * h : 64 * h + 4, :, :].bitcast(I32), rows.bitcast(I32))
+        for q in range(3):
+            nc.sync.dma_start(
+                xs_all[QUAD * q : QUAD * q + 4, :].bitcast(I32), xt_scales[0, 4 * q : 4 * q + 4, :].bitcast(I32)
+            )
+        nc.sync.dma_start(w_raw[:].bitcast(I32), w_words[0].rearrange("p n t -> p (n t)").bitcast(I32))
+        nc.sync.dma_start(xs_all[96:100, :].bitcast(I32), xt_scales[0, 12:16, :].bitcast(I32))
+        nc.sync.dma_start(idx2[:], offs2)
+
+        for t in range(2):
+            nc.vector.memset(boards[t][:], 0.0)
+        for t in range(2, PACK):
+            nc.gpsimd.memset(boards[t][:], 0.0)
+        nc.gpsimd.memset(vsc_all[:].bitcast(I32), 0)
+
+        nc.sync.dma_start(vs_all[:].bitcast(I32), vs_words[0].bitcast(I32))
+        for q in range(4):
+            nc.sync.dma_start(
+                vsc_all[QUAD * q : QUAD * q + 4, :].bitcast(I32), vs_scales[0, 4 * q : 4 * q + 4, :].bitcast(I32)
+            )
+        nc.sync.dma_start(idx3[:], offs3)
+        nc.sync.dma_start(idx4[:], offs4)
+
+        w_dealt = sb.tile([P, PACK, P], U32, name="w_dealt", align_bytes=64)
+        ws_dealt = sb.tile([P, PACK, P], U8, name="ws_dealt", align_bytes=64)
+        for h in range(2):
+            nc.vector.tensor_copy(
+                ws_raw[64 * h + QUAD : 64 * h + QUAD + 4, 0, :].bitcast(I32),
+                ws_raw[64 * h : 64 * h + 4, 1, :].bitcast(I32),
+            )
+        nc.vector.tensor_copy(
+            ws_dealt[:].rearrange("p t m -> p m t"), ws_raw[:, 0, :].rearrange("p (m t) -> p m t", t=PACK)
+        )
+        w_by_m = w_raw[:].rearrange("p (m t) -> p m t", t=PACK)
+        for pair in range(2):
+            ts = slice(2 * pair, 2 * pair + 2)
+            nc.scalar.copy(w_dealt[:, ts, :].rearrange("p t m -> p m t"), w_by_m[:, :, ts])
+
+        xg = sb.tile([P, J], U16, name="xg", tag="reuse2", align_bytes=64)
+        xgs = sb.tile([P, J], U8, name="xgs", tag="reuse3", align_bytes=64)
+
+        def first_product(acc, t, cols):
+            nc.tensor.matmul_mx(
+                out=acc,
+                lhsT=w_dealt[:, t, :].bitcast(E4M3),
+                lhsT_scale=ws_dealt[:, t, :],
+                rhs=xg[:, cols].bitcast(E2M1),
+                rhs_scale=xgs[:, cols],
+                start=True,
+                stop=True,
+            )
+
+        early = []
+        for h in range(2):
+            cols = slice(HALF * h, HALF * (h + 1))
+            entries = idx[:, 8 * h : 8 * h + 8]
+            nc.vector.tensor_copy(xg[:, cols], xt_all[:].indirect(entries))
+            nc.vector.tensor_copy(xgs[:, cols], xs_all[:].indirect(entries))
+            acc = psum.tile([P, 2, HALF], F32, name="acc_early%d" % h)
+            for t in range(2):
+                first_product(acc[:, t, :], t, cols)
+            hidden = sb.tile([P, 2, HALF], F32, name="hidden_early%d" % h)
+            if h == 0:
+                nc.scalar.copy(hidden[:], acc[:])
+            else:
+                nc.vector.tensor_copy(hidden[:], acc[:])
+            early.append(hidden)
+        late = []
+        for t in range(2, PACK):
+            acc = psum.tile([P, J], F32, name="acc_late%d" % t)
+            first_product(acc[:], t, slice(0, J))
+            hidden = sb.tile([P, J], F32, name="hidden_late%d" % t)
+            nc.vector.tensor_copy(hidden[:], acc[:])
+            late.append(hidden)
+
+        for h in range(2):
+            for t in range(2):
+                nc.scalar.activation(boards[t][:].indirect(idx2[:, 8 * h : 8 * h + 8]), early[h][:, t, :], COPY)
+        for t in range(2, PACK):
+            nc.scalar.activation(boards[t][:].indirect(idx2[:]), late[t - 2][:], COPY)
+
+        vg = sb.tile([P, U], U16, name="vg", align_bytes=64)
+        vgs = sb.tile([P, U], U8, name="vgs", align_bytes=64)
+        nc.vector.tensor_copy(vg[:], vs_all[:].indirect(idx3[:]))
+        nc.vector.tensor_copy(vgs[:], vsc_all[:].indirect(idx3[:]))
+
+        pages = [sb.tile([P, E], F32, name="page%d" % b, tag="reuse%d" % b, align_bytes=64) for b in range(4)]
+        for b in range(4):
+            nc.gpsimd.memset(pages[b][:], 0.0)
+
+        woven = sb.tile([P, C, PACK], BF16, name="woven", align_bytes=64)
+        codes = [sb.tile([P, P], U32, name="codes%d" % b, align_bytes=64) for b in range(4)]
+        scales = [sb.tile([P, P], U8, name="scales%d" % b, align_bytes=64) for b in range(4)]
+
+        def weave(t, cols):
+            nc.vector.tensor_copy(woven[:, cols, t], boards[t][:, cols])
+
+        for t in range(PACK - 1):
+            weave(t, slice(0, C))
+
+        accs = []
+        for pair in range(2):
+            for b in (2 * pair, 2 * pair + 1):
+                weave(PACK - 1, slice(P * b, P * (b + 1)))
+            for b in (2 * pair, 2 * pair + 1):
+                nc.vector.quantize_mx(
+                    out=codes[b][:].bitcast(E5M2), scales=scales[b][:], in_=woven[:, P * b : P * (b + 1), :].rearrange("p c t -> p (c t)")
+                )
+                acc = psum.tile([P, U], F32, name="acc_score%d" % b)
+                nc.tensor.matmul_mx(
+                    out=acc[:],
+                    lhsT=codes[b][:].bitcast(E5M2),
+                    lhsT_scale=scales[b][:],
+                    rhs=vg[:].bitcast(E2M1),
+                    rhs_scale=vgs[:],
+                    start=True,
+                    stop=True,
+                )
+                accs.append(acc)
+
+        scores = [sb.tile([P, U], F32, name="score%d" % b) for b in range(4)]
+        nc.scalar.copy(scores[0][:], accs[0][:])
+        nc.scalar.copy(scores[1][:], accs[1][:])
+        for b in range(4):
+            if b == 2:
+                nc.scalar.copy(scores[b][:], accs[b][:])
+            if b == 3:
+                nc.vector.tensor_copy(scores[b][:], accs[b][:])
+            if b % 2 == 0:
+                nc.scalar.activation(pages[b][:].indirect(idx4[:]), scores[b][:], COPY)
+            else:
+                nc.vector.tensor_copy(pages[b][:].indirect(idx4[:]), scores[b][:])
+            nc.sync.dma_start(out[P * b : P * (b + 1), :], pages[b][:])

@@ -39,26 +39,27 @@ def tile_list_pagequeries_kernel(
         xt_all = sb.tile([P, T], U16, name="xt_all", tag="reuse0", align_bytes=64)
         xs_all = sb.tile([P, T], U8, name="xs_all", tag="reuse1", align_bytes=64)
         w_raw = sb.tile([P, R], U32, name="w_raw", align_bytes=64)
-        ws_raw = sb.tile([P, 2, R], U8, name="ws_raw", align_bytes=64)
-        vs_all = sb.tile([P, S], U16, name="vs_all", align_bytes=64)
-        vsc_all = sb.tile([P, S], U8, name="vsc_all", align_bytes=64)
+        ws_rows = sb.tile([4, 4, R], U8, name="ws_rows", align_bytes=64)
+        ws_raw = sb.tile([P, R], U8, name="ws_raw", align_bytes=64)
+        vs_all = sb.tile([P, S], U16, name="vs_all", tag="store_words", align_bytes=64)
+        vsc_all = sb.tile([P, S], U8, name="vsc_all", tag="store_scales", align_bytes=64)
         boards = [sb.tile([P, C], F32, name="board%d" % t) for t in range(PACK)]
 
-        nc.gpsimd.memset(ws_raw[:, 0, :].bitcast(I32), 0)
         nc.vector.memset(xs_all[:].bitcast(I32), 0)
+        nc.vector.memset(ws_raw[:].bitcast(I32), 0)
+        nc.sync.dma_start(
+            ws_rows[:].bitcast(I32), w_scales[0].rearrange("(q r) c -> r q c", r=4).bitcast(I32)
+        )
 
         nc.sync.dma_start(idx[:], offs)
         nc.sync.dma_start(xt_all[:].bitcast(I32), xt_words[0].bitcast(I32))
-        for h in range(2):
-            rows = w_scales[0, 8 * h : 8 * h + 8, :].rearrange("(a r) c -> r a c", a=2)
-            nc.sync.dma_start(ws_raw[64 * h : 64 * h + 4, :, :].bitcast(I32), rows.bitcast(I32))
-        for q in range(3):
+        for q in range(4):
             nc.sync.dma_start(
                 xs_all[QUAD * q : QUAD * q + 4, :].bitcast(I32), xt_scales[0, 4 * q : 4 * q + 4, :].bitcast(I32)
             )
         nc.sync.dma_start(w_raw[:].bitcast(I32), w_words[0].rearrange("p n t -> p (n t)").bitcast(I32))
-        nc.sync.dma_start(xs_all[96:100, :].bitcast(I32), xt_scales[0, 12:16, :].bitcast(I32))
         nc.sync.dma_start(idx2[:], offs2)
+        nc.sync.dma_start(idx3[:], offs3)
 
         for t in range(2):
             nc.vector.memset(boards[t][:], 0.0)
@@ -71,20 +72,19 @@ def tile_list_pagequeries_kernel(
             nc.sync.dma_start(
                 vsc_all[QUAD * q : QUAD * q + 4, :].bitcast(I32), vs_scales[0, 4 * q : 4 * q + 4, :].bitcast(I32)
             )
-        nc.sync.dma_start(idx3[:], offs3)
         nc.sync.dma_start(idx4[:], offs4)
 
         w_dealt = sb.tile([P, PACK, P], U32, name="w_dealt", align_bytes=64)
         ws_dealt = sb.tile([P, PACK, P], U8, name="ws_dealt", align_bytes=64)
-        for h in range(2):
-            nc.vector.tensor_copy(
-                ws_raw[64 * h + QUAD : 64 * h + QUAD + 4, 0, :].bitcast(I32),
-                ws_raw[64 * h : 64 * h + 4, 1, :].bitcast(I32),
-            )
-        nc.vector.tensor_copy(
-            ws_dealt[:].rearrange("p t m -> p m t"), ws_raw[:, 0, :].rearrange("p (m t) -> p m t", t=PACK)
-        )
+        for q in range(4):
+            nc.vector.tensor_copy(ws_raw[QUAD * q : QUAD * q + 4, :].bitcast(I32), ws_rows[:, q, :].bitcast(I32))
         w_by_m = w_raw[:].rearrange("p (m t) -> p m t", t=PACK)
+        ws_by_m = ws_raw[:].rearrange("p (m t) -> p m t", t=PACK)
+
+        def deal_scales(ts):
+            nc.vector.tensor_copy(ws_dealt[:, ts, :].rearrange("p t m -> p m t"), ws_by_m[:, :, ts])
+
+        deal_scales(slice(0, 2))
         for pair in range(2):
             ts = slice(2 * pair, 2 * pair + 2)
             nc.scalar.copy(w_dealt[:, ts, :].rearrange("p t m -> p m t"), w_by_m[:, :, ts])
@@ -103,37 +103,46 @@ def tile_list_pagequeries_kernel(
                 stop=True,
             )
 
-        early = []
-        for h in range(2):
+        def gather_tokens(h):
             cols = slice(HALF * h, HALF * (h + 1))
             entries = idx[:, 8 * h : 8 * h + 8]
             nc.vector.tensor_copy(xg[:, cols], xt_all[:].indirect(entries))
             nc.vector.tensor_copy(xgs[:, cols], xs_all[:].indirect(entries))
-            acc = psum.tile([P, 2, HALF], F32, name="acc_early%d" % h)
-            for t in range(2):
-                first_product(acc[:, t, :], t, cols)
-            hidden = sb.tile([P, 2, HALF], F32, name="hidden_early%d" % h)
-            if h == 0:
+            return cols
+
+        cols = gather_tokens(0)
+        first = []
+        for t in range(2):
+            acc = psum.tile([P, HALF], F32, name="acc_first%d" % t)
+            first_product(acc[:], t, cols)
+            hidden = sb.tile([P, HALF], F32, name="hidden_first%d" % t)
+            if t == 0:
                 nc.scalar.copy(hidden[:], acc[:])
             else:
                 nc.vector.tensor_copy(hidden[:], acc[:])
-            early.append(hidden)
-        late = []
-        for t in range(2, PACK):
-            acc = psum.tile([P, J], F32, name="acc_late%d" % t)
-            first_product(acc[:], t, slice(0, J))
-            hidden = sb.tile([P, J], F32, name="hidden_late%d" % t)
-            nc.vector.tensor_copy(hidden[:], acc[:])
-            late.append(hidden)
+            first.append(hidden)
+        cols = gather_tokens(1)
+        acc = psum.tile([P, 2, HALF], F32, name="acc_second")
+        for t in range(2):
+            first_product(acc[:, t, :], t, cols)
+        second = sb.tile([P, 2, HALF], F32, name="hidden_second")
+        nc.vector.tensor_copy(second[:], acc[:])
+        deal_scales(slice(2, 4))
+        acc = psum.tile([P, 2, J], F32, name="acc_late")
+        for t in range(2):
+            first_product(acc[:, t, :], 2 + t, slice(0, J))
+        late = sb.tile([P, 2, J], F32, name="hidden_late")
+        nc.vector.tensor_copy(late[:], acc[:])
 
-        for h in range(2):
-            for t in range(2):
-                nc.scalar.activation(boards[t][:].indirect(idx2[:, 8 * h : 8 * h + 8]), early[h][:, t, :], COPY)
-        for t in range(2, PACK):
-            nc.scalar.activation(boards[t][:].indirect(idx2[:]), late[t - 2][:], COPY)
+        for t in range(2):
+            nc.scalar.activation(boards[t][:].indirect(idx2[:, 0:8]), first[t][:], COPY)
+        for t in range(2):
+            nc.scalar.activation(boards[t][:].indirect(idx2[:, 8:16]), second[:, t, :], COPY)
+        for t in range(2):
+            nc.scalar.activation(boards[2 + t][:].indirect(idx2[:]), late[:, t, :], COPY)
 
         vg = sb.tile([P, U], U16, name="vg", align_bytes=64)
-        vgs = sb.tile([P, U], U8, name="vgs", align_bytes=64)
+        vgs = sb.tile([P, U], U8, name="vgs", tag="store_words", align_bytes=64)
         nc.vector.tensor_copy(vg[:], vs_all[:].indirect(idx3[:]))
         nc.vector.tensor_copy(vgs[:], vsc_all[:].indirect(idx3[:]))
 
@@ -141,46 +150,49 @@ def tile_list_pagequeries_kernel(
         for b in range(4):
             nc.gpsimd.memset(pages[b][:], 0.0)
 
-        woven = sb.tile([P, C, PACK], BF16, name="woven", align_bytes=64)
+        woven = sb.tile([P, C, PACK], BF16, name="woven", tag="store_scales", align_bytes=64)
         codes = [sb.tile([P, P], U32, name="codes%d" % b, align_bytes=64) for b in range(4)]
         scales = [sb.tile([P, P], U8, name="scales%d" % b, align_bytes=64) for b in range(4)]
 
-        def weave(t, cols):
-            nc.vector.tensor_copy(woven[:, cols, t], boards[t][:, cols])
+        def weave(copy, t, cols):
+            copy(woven[:, cols, t], boards[t][:, cols])
 
-        for t in range(PACK - 1):
-            weave(t, slice(0, C))
-
+        blocks = [slice(P * b, P * (b + 1)) for b in range(4)]
+        for t in range(2):
+            weave(nc.vector.tensor_copy, t, slice(0, C))
+        weave(nc.vector.tensor_copy, 2, slice(0, 3 * P))
+        for t in range(2, PACK):
+            weave(nc.scalar.copy, t, blocks[3])
+        for b in range(2):
+            weave(nc.vector.tensor_copy, 3, blocks[b])
         accs = []
-        for pair in range(2):
-            for b in (2 * pair, 2 * pair + 1):
-                weave(PACK - 1, slice(P * b, P * (b + 1)))
-            for b in (2 * pair, 2 * pair + 1):
-                nc.vector.quantize_mx(
-                    out=codes[b][:].bitcast(E5M2), scales=scales[b][:], in_=woven[:, P * b : P * (b + 1), :].rearrange("p c t -> p (c t)")
-                )
-                acc = psum.tile([P, U], F32, name="acc_score%d" % b)
-                nc.tensor.matmul_mx(
-                    out=acc[:],
-                    lhsT=codes[b][:].bitcast(E5M2),
-                    lhsT_scale=scales[b][:],
-                    rhs=vg[:].bitcast(E2M1),
-                    rhs_scale=vgs[:],
-                    start=True,
-                    stop=True,
-                )
-                accs.append(acc)
+        for b in range(4):
+            nc.vector.quantize_mx(
+                out=codes[b][:].bitcast(E5M2),
+                scales=scales[b][:],
+                in_=woven[:, blocks[b], :].rearrange("p c t -> p (c t)"),
+            )
+            if b == 0:
+                weave(nc.vector.tensor_copy, 3, blocks[2])
+            acc = psum.tile([P, U], F32, name="acc_score%d" % b)
+            nc.tensor.matmul_mx(
+                out=acc[:],
+                lhsT=codes[b][:].bitcast(E5M2),
+                lhsT_scale=scales[b][:],
+                rhs=vg[:].bitcast(E2M1),
+                rhs_scale=vgs[:],
+                start=True,
+                stop=True,
+            )
+            accs.append(acc)
 
         scores = [sb.tile([P, U], F32, name="score%d" % b) for b in range(4)]
-        nc.scalar.copy(scores[0][:], accs[0][:])
-        nc.scalar.copy(scores[1][:], accs[1][:])
         for b in range(4):
-            if b == 2:
-                nc.scalar.copy(scores[b][:], accs[b][:])
-            if b == 3:
-                nc.vector.tensor_copy(scores[b][:], accs[b][:])
-            if b % 2 == 0:
+            copy = nc.scalar.copy if b < 2 else nc.vector.tensor_copy
+            copy(scores[b][:], accs[b][:])
+        for b in (0, 2, 1, 3):
+            if b < 2:
                 nc.scalar.activation(pages[b][:].indirect(idx4[:]), scores[b][:], COPY)
             else:
                 nc.vector.tensor_copy(pages[b][:].indirect(idx4[:]), scores[b][:])
-            nc.sync.dma_start(out[P * b : P * (b + 1), :], pages[b][:])
+            nc.sync.dma_start(out[blocks[b], :], pages[b][:])

@@ -36,8 +36,8 @@ def tile_list_pagequeries_kernel(
         idx3 = lists.tile([P, U // 16], U16, name="idx3")
         idx4 = lists.tile([P, U // 16], U16, name="idx4")
 
-        xt_all = sb.tile([P, T], U16, name="xt_all", tag="reuse0", align_bytes=64)
-        xs_all = sb.tile([P, T], U8, name="xs_all", tag="reuse1", align_bytes=64)
+        xt_all = sb.tile([P, T], U16, name="xt_all", align_bytes=64)
+        xs_all = sb.tile([P, T], U8, name="xs_all", align_bytes=64)
         w_raw = sb.tile([P, R], U32, name="w_raw", align_bytes=64)
         ws_rows = sb.tile([4, 4, R], U8, name="ws_rows", align_bytes=64)
         ws_raw = sb.tile([P, R], U8, name="ws_raw", align_bytes=64)
@@ -46,7 +46,7 @@ def tile_list_pagequeries_kernel(
         boards = [sb.tile([P, C], F32, name="board%d" % t) for t in range(PACK)]
 
         nc.vector.memset(xs_all[:].bitcast(I32), 0)
-        nc.vector.memset(ws_raw[:].bitcast(I32), 0)
+        nc.gpsimd.memset(ws_raw[:].bitcast(I32), 0)
         nc.sync.dma_start(
             ws_rows[:].bitcast(I32), w_scales[0].rearrange("(q r) c -> r q c", r=4).bitcast(I32)
         )
@@ -61,11 +61,10 @@ def tile_list_pagequeries_kernel(
         nc.sync.dma_start(idx2[:], offs2)
         nc.sync.dma_start(idx3[:], offs3)
 
-        for t in range(2):
-            nc.vector.memset(boards[t][:], 0.0)
-        for t in range(2, PACK):
-            nc.gpsimd.memset(boards[t][:], 0.0)
-        nc.gpsimd.memset(vsc_all[:].bitcast(I32), 0)
+        nc.vector.memset(vsc_all[:].bitcast(I32), 0)
+        for t in range(PACK):
+            engine = nc.vector if t < 2 else nc.gpsimd
+            engine.memset(boards[t][:].bitcast(I32), 0)
 
         nc.sync.dma_start(vs_all[:].bitcast(I32), vs_words[0].bitcast(I32))
         for q in range(4):
@@ -74,20 +73,25 @@ def tile_list_pagequeries_kernel(
             )
         nc.sync.dma_start(idx4[:], offs4)
 
-        w_dealt = sb.tile([P, PACK, P], U32, name="w_dealt", align_bytes=64)
-        ws_dealt = sb.tile([P, PACK, P], U8, name="ws_dealt", align_bytes=64)
+        w_dealt = [
+            sb.tile([P, 2, P], U32, name="w_dealt0", align_bytes=64),
+            sb.tile([P, 2, P], U32, name="w_dealt1", tag="reuse0", align_bytes=64),
+        ]
+        ws_dealt = [
+            sb.tile([P, 2, P], U8, name="ws_dealt0", align_bytes=64),
+            sb.tile([P, 2, P], U8, name="ws_dealt1", tag="reuse1", align_bytes=64),
+        ]
         for q in range(4):
             nc.vector.tensor_copy(ws_raw[QUAD * q : QUAD * q + 4, :].bitcast(I32), ws_rows[:, q, :].bitcast(I32))
         w_by_m = w_raw[:].rearrange("p (m t) -> p m t", t=PACK)
         ws_by_m = ws_raw[:].rearrange("p (m t) -> p m t", t=PACK)
 
-        def deal_scales(ts):
-            nc.vector.tensor_copy(ws_dealt[:, ts, :].rearrange("p t m -> p m t"), ws_by_m[:, :, ts])
+        def deal(copy, dealt, by_m, pair):
+            copy(dealt[pair][:].rearrange("p t m -> p m t"), by_m[:, :, 2 * pair : 2 * pair + 2])
 
-        deal_scales(slice(0, 2))
+        deal(nc.vector.tensor_copy, ws_dealt, ws_by_m, 0)
         for pair in range(2):
-            ts = slice(2 * pair, 2 * pair + 2)
-            nc.scalar.copy(w_dealt[:, ts, :].rearrange("p t m -> p m t"), w_by_m[:, :, ts])
+            deal(nc.scalar.copy, w_dealt, w_by_m, pair)
 
         xg = sb.tile([P, J], U16, name="xg", tag="reuse2", align_bytes=64)
         xgs = sb.tile([P, J], U8, name="xgs", tag="reuse3", align_bytes=64)
@@ -95,8 +99,8 @@ def tile_list_pagequeries_kernel(
         def first_product(acc, t, cols):
             nc.tensor.matmul_mx(
                 out=acc,
-                lhsT=w_dealt[:, t, :].bitcast(E4M3),
-                lhsT_scale=ws_dealt[:, t, :],
+                lhsT=w_dealt[t // 2][:, t % 2, :].bitcast(E4M3),
+                lhsT_scale=ws_dealt[t // 2][:, t % 2, :],
                 rhs=xg[:, cols].bitcast(E2M1),
                 rhs_scale=xgs[:, cols],
                 start=True,
@@ -127,7 +131,7 @@ def tile_list_pagequeries_kernel(
             first_product(acc[:, t, :], t, cols)
         second = sb.tile([P, 2, HALF], F32, name="hidden_second")
         nc.vector.tensor_copy(second[:], acc[:])
-        deal_scales(slice(2, 4))
+        deal(nc.vector.tensor_copy, ws_dealt, ws_by_m, 1)
         acc = psum.tile([P, 2, J], F32, name="acc_late")
         for t in range(2):
             first_product(acc[:, t, :], 2 + t, slice(0, J))
@@ -148,14 +152,14 @@ def tile_list_pagequeries_kernel(
 
         pages = [sb.tile([P, E], F32, name="page%d" % b, tag="reuse%d" % b, align_bytes=64) for b in range(4)]
         for b in range(4):
-            nc.gpsimd.memset(pages[b][:], 0.0)
+            nc.vector.memset(pages[b][:].bitcast(I32), 0)
 
-        woven = sb.tile([P, C, PACK], BF16, name="woven", tag="store_scales", align_bytes=64)
+        woven = sb.tile([P, C * PACK], BF16, name="woven", tag="store_scales", align_bytes=64)
         codes = [sb.tile([P, P], U32, name="codes%d" % b, align_bytes=64) for b in range(4)]
         scales = [sb.tile([P, P], U8, name="scales%d" % b, align_bytes=64) for b in range(4)]
 
         def weave(copy, t, cols):
-            copy(woven[:, cols, t], boards[t][:, cols])
+            copy(woven[:, PACK * cols.start + t : PACK * cols.stop : PACK], boards[t][:, cols])
 
         blocks = [slice(P * b, P * (b + 1)) for b in range(4)]
         for t in range(2):
@@ -165,12 +169,12 @@ def tile_list_pagequeries_kernel(
             weave(nc.scalar.copy, t, blocks[3])
         for b in range(2):
             weave(nc.vector.tensor_copy, 3, blocks[b])
-        accs = []
-        for b in range(4):
+        accs = {}
+        for b in (0, 1, 3, 2):
             nc.vector.quantize_mx(
                 out=codes[b][:].bitcast(E5M2),
                 scales=scales[b][:],
-                in_=woven[:, blocks[b], :].rearrange("p c t -> p (c t)"),
+                in_=woven[:, PACK * P * b : PACK * P * (b + 1)],
             )
             if b == 0:
                 weave(nc.vector.tensor_copy, 3, blocks[2])
@@ -184,15 +188,16 @@ def tile_list_pagequeries_kernel(
                 start=True,
                 stop=True,
             )
-            accs.append(acc)
+            accs[b] = acc
 
         scores = [sb.tile([P, U], F32, name="score%d" % b) for b in range(4)]
-        for b in range(4):
-            copy = nc.scalar.copy if b < 2 else nc.vector.tensor_copy
+        for b in (0, 1, 3, 2):
+            copy = nc.scalar.copy if b == 0 else nc.vector.tensor_copy
             copy(scores[b][:], accs[b][:])
-        for b in (0, 2, 1, 3):
+        for b in (0, 3, 1, 2):
             if b < 2:
                 nc.scalar.activation(pages[b][:].indirect(idx4[:]), scores[b][:], COPY)
             else:
                 nc.vector.tensor_copy(pages[b][:].indirect(idx4[:]), scores[b][:])
-            nc.sync.dma_start(out[blocks[b], :], pages[b][:])
+            queue = nc.scalar if b == 1 else nc.sync
+            queue.dma_start(out[blocks[b], :], pages[b][:])

@@ -37,16 +37,16 @@ def tile_list_pagequeries_kernel(
         idx4 = lists.tile([P, U // 16], U16, name="idx4")
 
         xt_all = sb.tile([P, T], U16, name="xt_all", align_bytes=64)
-        xs_all = sb.tile([P, T], U8, name="xs_all", align_bytes=64)
-        w_raw = sb.tile([P, R], U32, name="w_raw", align_bytes=64)
+        xs_all = sb.tile([P, T], U8, name="xs_all", tag="late2", align_bytes=64)
+        w_raw = sb.tile([P, R], U32, name="w_raw", tag="late3", align_bytes=64)
         ws_rows = sb.tile([4, 4, R], U8, name="ws_rows", align_bytes=64)
         ws_raw = sb.tile([P, R], U8, name="ws_raw", align_bytes=64)
         vs_all = sb.tile([P, S], U16, name="vs_all", tag="store_words", align_bytes=64)
         vsc_all = sb.tile([P, S], U8, name="vsc_all", tag="store_scales", align_bytes=64)
-        boards = [sb.tile([P, C], F32, name="board%d" % t) for t in range(PACK)]
+        boards = [sb.tile([P, C], F32, name="board%d" % t) for t in range(2)]
 
         nc.vector.memset(xs_all[:].bitcast(I32), 0)
-        nc.gpsimd.memset(ws_raw[:].bitcast(I32), 0)
+        nc.vector.memset(ws_raw[:].bitcast(I32), 0)
         nc.sync.dma_start(
             ws_rows[:].bitcast(I32), w_scales[0].rearrange("(q r) c -> r q c", r=4).bitcast(I32)
         )
@@ -62,9 +62,8 @@ def tile_list_pagequeries_kernel(
         nc.sync.dma_start(idx3[:], offs3)
 
         nc.vector.memset(vsc_all[:].bitcast(I32), 0)
-        for t in range(PACK):
-            engine = nc.vector if t < 2 else nc.gpsimd
-            engine.memset(boards[t][:].bitcast(I32), 0)
+        for t in range(2):
+            nc.vector.memset(boards[t][:].bitcast(I32), 0)
 
         nc.sync.dma_start(vs_all[:].bitcast(I32), vs_words[0].bitcast(I32))
         for q in range(4):
@@ -137,6 +136,10 @@ def tile_list_pagequeries_kernel(
             first_product(acc[:, t, :], 2 + t, slice(0, J))
         late = sb.tile([P, 2, J], F32, name="hidden_late")
         nc.vector.tensor_copy(late[:], acc[:])
+
+        for t in range(2, PACK):
+            boards.append(sb.tile([P, C], F32, name="board%d" % t, tag="late%d" % t, align_bytes=64))
+            nc.vector.memset(boards[t][:].bitcast(I32), 0)
 
         for t in range(2):
             nc.scalar.activation(boards[t][:].indirect(idx2[:, 0:8]), first[t][:], COPY)

@@ -37,8 +37,8 @@ def tile_list_pagequeries_kernel(
         idx4 = lists.tile([P, U // 16], U16, name="idx4")
 
         xt_all = sb.tile([P, T], U16, name="xt_all", align_bytes=64)
-        xs_all = sb.tile([P, T], U8, name="xs_all", tag="late2", align_bytes=64)
-        w_raw = sb.tile([P, R], U32, name="w_raw", tag="late3", align_bytes=64)
+        xs_all = sb.tile([P, T], U8, name="xs_all", align_bytes=64)
+        w_raw = sb.tile([P, R], U32, name="w_raw", align_bytes=64)
         ws_rows = sb.tile([4, 4, R], U8, name="ws_rows", align_bytes=64)
         ws_raw = sb.tile([P, R], U8, name="ws_raw", align_bytes=64)
         vs_all = sb.tile([P, S], U16, name="vs_all", tag="store_words", align_bytes=64)
@@ -73,12 +73,12 @@ def tile_list_pagequeries_kernel(
         nc.sync.dma_start(idx4[:], offs4)
 
         w_dealt = [
-            sb.tile([P, 2, P], U32, name="w_dealt0", align_bytes=64),
-            sb.tile([P, 2, P], U32, name="w_dealt1", tag="reuse0", align_bytes=64),
+            sb.tile([P, 2, P], U32, name="w_dealt0", tag="late2", align_bytes=64),
+            sb.tile([P, 2, P], U32, name="w_dealt1", tag="page0", align_bytes=64),
         ]
         ws_dealt = [
-            sb.tile([P, 2, P], U8, name="ws_dealt0", align_bytes=64),
-            sb.tile([P, 2, P], U8, name="ws_dealt1", tag="reuse1", align_bytes=64),
+            sb.tile([P, 2, P], U8, name="ws_dealt0", tag="late3", align_bytes=64),
+            sb.tile([P, 2, P], U8, name="ws_dealt1", tag="page3", align_bytes=64),
         ]
         for q in range(4):
             nc.vector.tensor_copy(ws_raw[QUAD * q : QUAD * q + 4, :].bitcast(I32), ws_rows[:, q, :].bitcast(I32))
@@ -92,8 +92,8 @@ def tile_list_pagequeries_kernel(
         for pair in range(2):
             deal(nc.scalar.copy, w_dealt, w_by_m, pair)
 
-        xg = sb.tile([P, J], U16, name="xg", tag="reuse2", align_bytes=64)
-        xgs = sb.tile([P, J], U8, name="xgs", tag="reuse3", align_bytes=64)
+        xg = sb.tile([P, J], U16, name="xg", align_bytes=64)
+        xgs = sb.tile([P, J], U8, name="xgs", align_bytes=64)
 
         def first_product(acc, t, cols):
             nc.tensor.matmul_mx(
@@ -153,12 +153,13 @@ def tile_list_pagequeries_kernel(
         nc.vector.tensor_copy(vg[:], vs_all[:].indirect(idx3[:]))
         nc.vector.tensor_copy(vgs[:], vsc_all[:].indirect(idx3[:]))
 
-        pages = [sb.tile([P, E], F32, name="page%d" % b, tag="reuse%d" % b, align_bytes=64) for b in range(4)]
-        for b in range(4):
+        pages = {}
+        for b in (0, 3):
+            pages[b] = sb.tile([P, E], F32, name="page%d" % b, tag="page%d" % b, align_bytes=64)
             nc.vector.memset(pages[b][:].bitcast(I32), 0)
 
         woven = sb.tile([P, C * PACK], BF16, name="woven", tag="store_scales", align_bytes=64)
-        codes = [sb.tile([P, P], U32, name="codes%d" % b, align_bytes=64) for b in range(4)]
+        codes = [sb.tile([P, P], U32, name="codes%d" % b, tag="codes%d" % b, align_bytes=64) for b in range(4)]
         scales = [sb.tile([P, P], U8, name="scales%d" % b, align_bytes=64) for b in range(4)]
 
         def weave(copy, t, cols):
@@ -192,6 +193,10 @@ def tile_list_pagequeries_kernel(
                 stop=True,
             )
             accs[b] = acc
+
+        for b, tag in ((1, "store_scales"), (2, "codes2")):
+            pages[b] = sb.tile([P, E], F32, name="page%d" % b, tag=tag, align_bytes=64)
+            nc.gpsimd.memset(pages[b][:].bitcast(I32), 0)
 
         scores = [sb.tile([P, U], F32, name="score%d" % b) for b in range(4)]
         for b in (0, 1, 3, 2):

from contextlib import ExitStack

import concourse.mybir as mybir

K, T, J, R, C, S, U, E = 512, 1024, 256, 512, 512, 1024, 256, 512
FLOPS = 2 * K * R * J + 2 * R * C * U

F32 = mybir.dt.float32
BF16 = mybir.dt.bfloat16
I32 = mybir.dt.int32
U32 = mybir.dt.uint32
U16 = mybir.dt.uint16
U8 = mybir.dt.uint8
E4M3 = mybir.dt.float8_e4m3fn_x4
E5M2 = mybir.dt.float8_e5m2_x4
E2M1 = mybir.dt.float4_e2m1fn_x4
COPY = mybir.ActivationFunctionType.Copy

P = 128
PACK = 4
QUAD = 32
HALF = J // 2


def tile_list_pagequeries_kernel(
    tc, xt_words, xt_scales, w_words, w_scales, vs_words, vs_scales, offs, offs2, offs3, offs4, out
):
    nc = tc.nc
    with ExitStack() as ctx:
        lists = ctx.enter_context(tc.tile_pool(name="lists", bufs=1))
        sb = ctx.enter_context(tc.tile_pool(name="sb", bufs=1))
        psum = ctx.enter_context(tc.psum_pool(name="psum", bufs=1))

        idx = lists.tile([P, J // 16], U16, name="idx")
        idx2 = lists.tile([P, J // 16], U16, name="idx2")
        idx3 = lists.tile([P, U // 16], U16, name="idx3")
        idx4 = lists.tile([P, U // 16], U16, name="idx4")

        xt_all = sb.tile([P, T], U16, name="xt_all", align_bytes=64)
        xs_all = sb.tile([P, T], U8, name="xs_all", align_bytes=64)
        w_raw = sb.tile([P, R], U32, name="w_raw", align_bytes=64)
        ws_rows = sb.tile([4, 4, R], U8, name="ws_rows", align_bytes=64)
        ws_raw = sb.tile([P, R], U8, name="ws_raw", align_bytes=64)
        vs_all = sb.tile([P, S], U16, name="vs_all", tag="store_words", align_bytes=64)
        vsc_all = sb.tile([P, S], U8, name="vsc_all", tag="store_scales", align_bytes=64)
        boards = [sb.tile([P, C], F32, name="board%d" % t) for t in range(2)]

        nc.vector.memset(xs_all[:].bitcast(I32), 0)
        nc.vector.memset(ws_raw[:].bitcast(I32), 0)
        nc.sync.dma_start(
            ws_rows[:].bitcast(I32), w_scales[0].rearrange("(q r) c -> r q c", r=4).bitcast(I32)
        )

        nc.sync.dma_start(idx[:], offs)
        nc.sync.dma_start(xt_all[:].bitcast(I32), xt_words[0].bitcast(I32))
        for q in range(4):
            nc.sync.dma_start(
                xs_all[QUAD * q : QUAD * q + 4, :].bitcast(I32), xt_scales[0, 4 * q : 4 * q + 4, :].bitcast(I32)
            )
        nc.sync.dma_start(w_raw[:].bitcast(I32), w_words[0].rearrange("p n t -> p (n t)").bitcast(I32))
        nc.sync.dma_start(idx2[:], offs2)
        nc.sync.dma_start(idx3[:], offs3)

        nc.vector.memset(vsc_all[:].bitcast(I32), 0)
        for t in range(2):
            nc.vector.memset(boards[t][:].bitcast(I32), 0)

        nc.sync.dma_start(vs_all[:].bitcast(I32), vs_words[0].bitcast(I32))
        for q in range(4):
            nc.sync.dma_start(
                vsc_all[QUAD * q : QUAD * q + 4, :].bitcast(I32), vs_scales[0, 4 * q : 4 * q + 4, :].bitcast(I32)
            )
        nc.sync.dma_start(idx4[:], offs4)

        w_dealt = [
            sb.tile([P, 2, P], U32, name="w_dealt0", tag="late2", align_bytes=64),
            sb.tile([P, 2, P], U32, name="w_dealt1", tag="page0", align_bytes=64),
        ]
        ws_dealt = [
            sb.tile([P, 2, P], U8, name="ws_dealt0", tag="late3", align_bytes=64),
            sb.tile([P, 2, P], U8, name="ws_dealt1", tag="page3", align_bytes=64),
        ]
        for q in range(4):
            nc.vector.tensor_copy(ws_raw[QUAD * q : QUAD * q + 4, :].bitcast(I32), ws_rows[:, q, :].bitcast(I32))
        w_by_m = w_raw[:].rearrange("p (m t) -> p m t", t=PACK)
        ws_by_m = ws_raw[:].rearrange("p (m t) -> p m t", t=PACK)

        def deal(copy, dealt, by_m, pair):
            copy(dealt[pair][:].rearrange("p t m -> p m t"), by_m[:, :, 2 * pair : 2 * pair + 2])

        deal(nc.vector.tensor_copy, ws_dealt, ws_by_m, 0)
        for pair in range(2):
            deal(nc.scalar.copy, w_dealt, w_by_m, pair)

        xg = sb.tile([P, J], U16, name="xg", align_bytes=64)
        xgs = sb.tile([P, J], U8, name="xgs", align_bytes=64)

        def first_product(acc, t, cols):
            nc.tensor.matmul_mx(
                out=acc,
                lhsT=w_dealt[t // 2][:, t % 2, :].bitcast(E4M3),
                lhsT_scale=ws_dealt[t // 2][:, t % 2, :],
                rhs=xg[:, cols].bitcast(E2M1),
                rhs_scale=xgs[:, cols],
                start=True,
                stop=True,
            )

        def gather_tokens(h):
            cols = slice(HALF * h, HALF * (h + 1))
            entries = idx[:, 8 * h : 8 * h + 8]
            nc.vector.tensor_copy(xg[:, cols], xt_all[:].indirect(entries))
            nc.vector.tensor_copy(xgs[:, cols], xs_all[:].indirect(entries))
            return cols

        cols = gather_tokens(0)
        first = []
        for t in range(2):
            acc = psum.tile([P, HALF], F32, name="acc_first%d" % t)
            first_product(acc[:], t, cols)
            hidden = sb.tile([P, HALF], F32, name="hidden_first%d" % t)
            if t == 0:
                nc.scalar.copy(hidden[:], acc[:])
            else:
                nc.vector.tensor_copy(hidden[:], acc[:])
            first.append(hidden)
        cols = gather_tokens(1)
        acc = psum.tile([P, 2, HALF], F32, name="acc_second")
        for t in range(2):
            first_product(acc[:, t, :], t, cols)
        second = sb.tile([P, 2, HALF], F32, name="hidden_second")
        nc.vector.tensor_copy(second[:], acc[:])
        deal(nc.vector.tensor_copy, ws_dealt, ws_by_m, 1)
        acc = psum.tile([P, 2, J], F32, name="acc_late")
        for t in range(2):
            first_product(acc[:, t, :], 2 + t, slice(0, J))
        late = sb.tile([P, 2, J], F32, name="hidden_late")
        nc.vector.tensor_copy(late[:], acc[:])

        for t in range(2, PACK):
            boards.append(sb.tile([P, C], F32, name="board%d" % t, tag="late%d" % t, align_bytes=64))
            nc.vector.memset(boards[t][:].bitcast(I32), 0)

        for t in range(2):
            nc.scalar.activation(boards[t][:].indirect(idx2[:, 0:8]), first[t][:], COPY)
        for t in range(2):
            nc.scalar.activation(boards[t][:].indirect(idx2[:, 8:16]), second[:, t, :], COPY)
        for t in range(2):
            nc.scalar.activation(boards[2 + t][:].indirect(idx2[:]), late[:, t, :], COPY)

        vg = sb.tile([P, U], U16, name="vg", align_bytes=64)
        vgs = sb.tile([P, U], U8, name="vgs", tag="store_words", align_bytes=64)
        nc.vector.tensor_copy(vg[:], vs_all[:].indirect(idx3[:]))
        nc.vector.tensor_copy(vgs[:], vsc_all[:].indirect(idx3[:]))

        pages = {}
        for b in (0, 3):
            pages[b] = sb.tile([P, E], F32, name="page%d" % b, tag="page%d" % b, align_bytes=64)
            nc.vector.memset(pages[b][:].bitcast(I32), 0)

        woven = sb.tile([P, C * PACK], BF16, name="woven", tag="store_scales", align_bytes=64)
        codes = [sb.tile([P, P], U32, name="codes%d" % b, tag="codes%d" % b, align_bytes=64) for b in range(4)]
        scales = [sb.tile([P, P], U8, name="scales%d" % b, align_bytes=64) for b in range(4)]

        def weave(copy, t, cols):
            copy(woven[:, PACK * cols.start + t : PACK * cols.stop : PACK], boards[t][:, cols])

        blocks = [slice(P * b, P * (b + 1)) for b in range(4)]
        for t in range(2):
            weave(nc.vector.tensor_copy, t, slice(0, C))
        weave(nc.vector.tensor_copy, 2, slice(0, 3 * P))
        for t in range(2, PACK):
            weave(nc.scalar.copy, t, blocks[3])
        for b in range(2):
            weave(nc.vector.tensor_copy, 3, blocks[b])
        accs = {}
        for b in (0, 1, 3, 2):
            nc.vector.quantize_mx(
                out=codes[b][:].bitcast(E5M2),
                scales=scales[b][:],
                in_=woven[:, PACK * P * b : PACK * P * (b + 1)],
            )
            if b == 0:
                weave(nc.vector.tensor_copy, 3, blocks[2])
            acc = psum.tile([P, U], F32, name="acc_score%d" % b)
            nc.tensor.matmul_mx(
                out=acc[:],
                lhsT=codes[b][:].bitcast(E5M2),
                lhsT_scale=scales[b][:],
                rhs=vg[:].bitcast(E2M1),
                rhs_scale=vgs[:],
                start=True,
                stop=True,
            )
            accs[b] = acc

        for b, tag in ((1, "store_scales"), (2, "codes2")):
            pages[b] = sb.tile([P, E], F32, name="page%d" % b, tag=tag, align_bytes=64)
            nc.gpsimd.memset(pages[b][:].bitcast(I32), 0)

        scores = [sb.tile([P, U], F32, name="score%d" % b) for b in range(4)]
        for b in (0, 1, 3, 2):
            copy = nc.scalar.copy if b == 0 else nc.vector.tensor_copy
            copy(scores[b][:], accs[b][:])
        for b in (0, 3, 1, 2):
            if b < 2:
                nc.scalar.activation(pages[b][:].indirect(idx4[:]), scores[b][:], COPY)
            else:
                nc.vector.tensor_copy(pages[b][:].indirect(idx4[:]), scores[b][:])
            queue = nc.scalar if b == 1 else nc.sync
            queue.dma_start(out[blocks[b], :], pages[b][:])
